import numpy as np
import ml_dtypes


def mxq(x, axis, fmt="e4m3"):
    dtype, down = {"e4m3": (ml_dtypes.float8_e4m3fn, 7), "e5m2": (ml_dtypes.float8_e5m2, 14)}[fmt]
    v = np.moveaxis(np.asarray(x, np.float32).astype(ml_dtypes.bfloat16).astype(np.float64), axis, -1)
    blocks = v.reshape(v.shape[:-1] + (-1, 32))
    amax = np.abs(blocks).max(-1, keepdims=True)
    byte = np.maximum(np.where(amax > 0, np.frexp(amax)[1] - 1 + 127, 0) - down, 1)
    scale = np.exp2(byte - 127.0)
    codes = (blocks / scale).astype(np.float32).astype(dtype).astype(np.float64)
    return np.moveaxis((codes * scale).reshape(v.shape), -1, axis)


WIDE = False


def mx_kscale(k):
    if not WIDE:
        return np.ones(k)
    levels = np.array([10, -10, 5, -5, 0])
    if k % 512:
        return np.exp2(np.random.permutation(np.resize(levels, k // 32))).repeat(32)
    a = np.empty((k // 512, 16))
    for p in range(k // 512):
        a[p, :8] = np.random.permutation(np.resize(levels, 8))
        for g in range(8):
            far = levels[np.abs(levels - a[p, g]) >= 10]
            a[p, g + 8] = far[np.random.randint(len(far))]
    return np.exp2(a.ravel()).repeat(32)


def f64(x):
    return np.asarray(x).astype(np.float64)


def striped(idx):
    return np.tile(idx.reshape(-1, 16).T, (8, 1)).astype(np.uint16)


def unstriped(offs):
    return offs[:16].T.reshape(-1).astype(np.int64)


def striped8(idx):
    return np.concatenate([x.reshape(-1, 16).T for x in idx]).astype(np.uint16)


def runs(offs, k):
    lists = np.stack([offs[16 * r : 16 * r + 16].T.reshape(-1) for r in range(8)]).astype(np.int64)
    return lists[np.arange(k) % 512 // 64]


def pack_weight(w):
    k, n = w.shape
    w = f64(np.asarray(w, np.float32).astype(ml_dtypes.bfloat16)).reshape(k // 32, 32, n)
    amax = np.abs(w).max(1)
    byte = np.clip(np.where(amax > 0, np.frexp(amax)[1] - 1 + 127 - 7, 1), 1, 254)
    scaled = (w * np.exp2(127.0 - byte)[:, None, :]).reshape(k, n).astype(np.float32)
    words = np.ascontiguousarray(scaled.reshape(k // 512, 128, 4, n).transpose(0, 1, 3, 2)).astype(ml_dtypes.float8_e4m3fn).view(np.uint8)
    return words, np.ascontiguousarray(byte.astype(np.uint8).reshape(k // 512, 16, n))


def unpack_weight(words, scales):
    g, p, n, _ = words.shape
    vals = np.ascontiguousarray(words).view(ml_dtypes.float8_e4m3fn).astype(np.float64) * np.repeat(np.exp2(scales.astype(np.float64) - 127.0), 8, axis=1)[..., None]
    return vals.transpose(0, 1, 3, 2).reshape(g * 512, n)


E2M1 = np.array([0.0, 0.5, 1.0, 1.5, 2.0, 3.0, 4.0, 6.0, -0.0, -0.5, -1.0, -1.5, -2.0, -3.0, -4.0, -6.0])


def pack_fp4(w):
    k, n = w.shape
    w = f64(np.asarray(w, np.float32).astype(ml_dtypes.bfloat16)).reshape(k // 32, 32, n)
    amax = np.abs(w).max(1)
    mant, ex = np.frexp(amax / 6.0)
    byte = np.clip(np.where(amax > 0, np.where(mant > 0.5, ex, ex - 1) + 127, 1), 1, 254)
    scaled = (w * np.exp2(127.0 - byte)[:, None, :]).reshape(k, n).astype(np.float32)
    c = np.ascontiguousarray(scaled.reshape(k // 512, 128, 4, n).transpose(0, 1, 3, 2)).astype(ml_dtypes.float4_e2m1fn).view(np.uint8) & 0xF
    words = (c[..., 0::2] | (c[..., 1::2] << 4)).reshape(k // 512, 128, 2 * n)
    return np.ascontiguousarray(words), np.ascontiguousarray(byte.astype(np.uint8).reshape(k // 512, 16, n))


def unpack_fp4(words, scales):
    g, _, n = scales.shape
    words = np.ascontiguousarray(words).reshape(g, 128, n, 2)
    nib = np.empty((g, 128, n, 4), np.uint8)
    nib[..., 0::2] = words & 0xF
    nib[..., 1::2] = words >> 4
    vals = E2M1[nib] * np.repeat(np.exp2(scales.astype(np.float64) - 127.0), 8, axis=1)[..., None]
    return vals.transpose(0, 1, 3, 2).reshape(g * 512, n)


def planes(y):
    n, m = y.shape
    v = y.astype(np.float32).astype(ml_dtypes.bfloat16).astype(np.float64).reshape(n // 32, 32, m)
    top = np.abs(v).max(1)
    byte = np.clip(np.where(top > 0, np.frexp(top)[1] - 1 + 127 - 7, 1), 1, 254)
    codes = (v * np.exp2(127.0 - byte)[:, None, :]).reshape(n, m).astype(np.float32).astype(ml_dtypes.float8_e4m3fn).view(np.uint8)
    words = codes.reshape(n // 512, 128, 4, m).transpose(0, 1, 3, 2)
    return np.ascontiguousarray(words), np.ascontiguousarray(byte.astype(np.uint8).reshape(n // 512, 16, m))


K, T, S, N, H = 512, 2048, 512, 512, 512


def setup_inputs():
    n = np.random.standard_normal
    s = mx_kscale(K)[:, None]
    u = mx_kscale(H)
    packed_xT = pack_weight(n((K, T)) * s)
    packed_w1 = pack_fp4(n((K, H)) / np.sqrt(K) / s)
    packed_w2 = pack_fp4(n((H, N)) / np.sqrt(H) / u[:, None])
    return {
        "x_words": packed_xT[0],
        "x_scales": packed_xT[1],
        "w1_words": packed_w1[0],
        "w1_scales": packed_w1[1],
        "gn": (np.random.uniform(0.5, 1.5, (H, 1)) * u[:, None]).astype(np.float32),
        "w2_words": packed_w2[0],
        "w2_scales": packed_w2[1],
        "res": (2 * n((N, S))).astype(np.float32),
        "offs": striped(np.random.permutation(T)[:S]),
        "rt": striped8(np.stack([np.random.permutation(S) for _ in range(8)])),
        "lf": striped8(np.stack([np.random.permutation(S) for _ in range(8)])),
    }


def reference(x_words, x_scales, w1_words, w1_scales, gn, w2_words, w2_scales, res, offs, rt, lf):
    xq = unpack_weight(x_words, x_scales)[:, unstriped(offs)]
    y = unpack_fp4(w1_words, w1_scales).T @ xq
    d = y[np.arange(H)[:, None], runs(rt, H)] - y
    p = d / (np.sqrt((d) ** 2 + 1))
    z = f64(gn) * (p - (p[np.arange(H)[:, None], runs(lf, H)]))
    out_0 = f64(res) + (unpack_fp4(w2_words, w2_scales).T @ mxq(z, 0, "e4m3"))
    return (out_0,) + planes(out_0)

@@ -1,0 +1,191 @@
+from contextlib import ExitStack
+
+import concourse.mybir as mybir
+
+K, T, S, N, H = 512, 2048, 512, 512, 512
+FLOPS = 2 * K * H * S + 2 * H * N * S
+
+F32 = mybir.dt.float32
+BF16 = mybir.dt.bfloat16
+I32 = mybir.dt.int32
+U32 = mybir.dt.uint32
+U16 = mybir.dt.uint16
+U8 = mybir.dt.uint8
+FP8X4 = mybir.dt.float8_e4m3fn_x4
+FP4X4 = mybir.dt.float4_e2m1fn_x4
+ALU = mybir.AluOpType
+ACT = mybir.ActivationFunctionType
+
+P = 128
+PACK = 4
+HALF = 256
+CHUNK = 128
+
+
+def tile_picked_curvflow_none_po_kernel(tc, x_words, x_scales, w1_words, w1_scales, gn, w2_words, w2_scales, res, offs, rt, lf, out_0, out_1, out_2):
+    nc = tc.nc
+    with ExitStack() as ctx:
+        lists = ctx.enter_context(tc.tile_pool(name="lists", bufs=1))
+        sb = ctx.enter_context(tc.tile_pool(name="sb", bufs=1))
+        psum = ctx.enter_context(tc.psum_pool(name="psum", bufs=1))
+
+        offs_sb = lists.tile([P, S // 16], U16, name="offs_sb")
+        rt_sb = lists.tile([P, S // 16], U16, name="rt_sb")
+        lf_sb = lists.tile([P, S // 16], U16, name="lf_sb")
+
+        xw = sb.tile([P, T], U32, name="xw", tag="big", align_bytes=64)
+        xs = sb.tile([P, T], U8, name="xs", align_bytes=64)
+        ww_raw = sb.tile([P, 2 * H], U8, name="ww_raw", align_bytes=64)
+        ws_raw = sb.tile([P, H], U8, name="ws_raw", align_bytes=64)
+        gain = sb.tile([P, PACK], F32, name="gain")
+        warm_in = sb.tile([P, 1], F32, name="warm_in")
+        warm_out = sb.tile([P, 1], F32, name="warm_out")
+
+        def load_scales(queues, tile, src):
+            for q, queue in enumerate(queues):
+                queue.dma_start(tile[32 * q : 32 * q + 4, :].bitcast(I32), src[0, 4 * q : 4 * q + 4, :].bitcast(I32))
+
+        nc.vector.memset(xs[:].bitcast(I32), 0)
+        nc.gpsimd.memset(ws_raw[:].bitcast(I32), 0)
+        nc.vector.memset(warm_in[:], 1.0)
+
+        nc.sync.dma_start(offs_sb[:], offs)
+        nc.sync.dma_start(rt_sb[:], rt)
+        nc.sync.dma_start(lf_sb[:], lf)
+        nc.sync.dma_start(xw[:].bitcast(I32), x_words[0].rearrange("p c r -> p (c r)").bitcast(I32))
+        nc.sync.dma_start(ww_raw[:].bitcast(I32), w1_words[0].bitcast(I32))
+        load_scales([nc.scalar] * 4, xs, x_scales)
+        load_scales([nc.gpsimd, nc.gpsimd, nc.scalar, nc.scalar], ws_raw, w1_scales)
+        nc.gpsimd.dma_start(gain[:], gn.rearrange("(p t) o -> p (t o)", t=PACK))
+        nc.scalar.activation(warm_out[:], warm_in[:], ACT.Abs_reciprocal_sqrt)
+
+        def deal(words_raw, scales_raw, name):
+            words = sb.tile([P, 2 * H], U8, name=name + "w", align_bytes=64)
+            scales = sb.tile([P, H], U8, name=name + "s", align_bytes=64)
+            nc.vector.tensor_copy(words[:].rearrange("p (t m b) -> p m t b", t=PACK, b=2), words_raw[:].rearrange("p (m t b) -> p m t b", t=PACK, b=2))
+            nc.vector.tensor_copy(scales[:].rearrange("p (t m) -> p m t", t=PACK), scales_raw[:].rearrange("p (m t) -> p m t", t=PACK))
+            return words, scales
+
+        xg = sb.tile([P, S], U32, name="xg", align_bytes=64)
+        xgs = sb.tile([P, S], U8, name="xgs", align_bytes=64)
+        w1w, w1s = deal(ww_raw, ws_raw, "w1")
+        nc.vector.tensor_copy(xgs[:], xs[:].indirect(offs_sb[:]))
+        nc.vector.tensor_copy(xg[:], xw[:].indirect(offs_sb[:]))
+
+        nc.sync.dma_start(ww_raw[:].bitcast(I32), w2_words[0].bitcast(I32))
+        load_scales([nc.sync] * 4, ws_raw, w2_scales)
+        res_sb = sb.tile([P, PACK, S], F32, name="res_sb", tag="big", align_bytes=64)
+        nc.sync.dma_start(res_sb[:], res.rearrange("(p t) j -> p t j", t=PACK))
+
+        y_ps = [psum.tile([P, S], F32, name=f"y_ps{t}") for t in range(PACK)]
+        for t in range(PACK):
+            nc.tensor.matmul_mx(
+                out=y_ps[t][:],
+                lhsT=w1w[:, 2 * P * t : 2 * P * (t + 1)].bitcast(FP4X4),
+                lhsT_scale=w1s[:, P * t : P * (t + 1)],
+                rhs=xg[:].bitcast(FP8X4),
+                rhs_scale=xgs[:],
+                start=True,
+                stop=True,
+            )
+
+        neg_gain = sb.tile([P, PACK], F32, name="neg_gain")
+        nc.vector.tensor_scalar(neg_gain[:], gain[:], -1.0, None, ALU.mult)
+
+        y_win = [sb.tile([P, S], F32, name=f"y_win{t}") for t in range(PACK)]
+        y_own = [sb.tile([P, S], F32, name=f"y_own{t}") for t in range(PACK)]
+        d = [sb.tile([P, S], F32, name=f"d{t}") for t in range(PACK)]
+        sq = [sb.tile([P, S], F32, name=f"sq{t}") for t in range(PACK)]
+        r = [sb.tile([P, S], F32, name=f"r{t}") for t in range(PACK)]
+        p_win = [sb.tile([P, S], F32, name=f"p_win{t}") for t in range(PACK)]
+        p_own = [sb.tile([P, S], F32, name=f"p_own{t}") for t in range(PACK)]
+        z = [sb.tile([P, PACK, CHUNK], F32, name=f"z{c}") for c in range(S // CHUNK)]
+
+        def leave_psum(t):
+            nc.scalar.copy(y_win[t][:], y_ps[t][:])
+            nc.scalar.copy(y_own[t][:], y_ps[t][:])
+
+        def difference(t):
+            for h in range(S // HALF):
+                cols = slice(h * HALF, (h + 1) * HALF)
+                nc.vector.tensor_tensor(d[t][:, cols], y_win[t][:].indirect(rt_sb[:, h * HALF // 16 : (h + 1) * HALF // 16]), y_own[t][:, cols], ALU.subtract)
+
+        def root(t):
+            nc.scalar.activation(sq[t][:], d[t][:], ACT.Square)
+            nc.scalar.activation(r[t][:], sq[t][:], ACT.Abs_reciprocal_sqrt, bias=1.0)
+
+        def slope(t):
+            nc.vector.scalar_tensor_tensor(p_win[t][:], d[t][:], neg_gain[:, t : t + 1], r[t][:], ALU.mult, ALU.mult)
+            nc.scalar.copy(p_own[t][:], p_win[t][:])
+
+        def curvature(t, c):
+            cols = slice(c * CHUNK, (c + 1) * CHUNK)
+            nc.vector.tensor_tensor(z[c][:, t, :], p_win[t][:].indirect(lf_sb[:, c * CHUNK // 16 : (c + 1) * CHUNK // 16]), p_own[t][:, cols], ALU.subtract)
+
+        chunks = range(S // CHUNK)
+        for step in range(PACK + 2):
+            if step < PACK:
+                leave_psum(step)
+                difference(step)
+            if 1 <= step <= PACK:
+                root(step - 1)
+                slope(step - 1)
+            if step == 2:
+                w2w, w2s = deal(ww_raw, ws_raw, "w2")
+            if 2 <= step <= PACK:
+                for c in chunks:
+                    curvature(step - 2, c)
+
+        out_scales = sb.tile([P, S], U8, name="out_scales", align_bytes=64)
+        out0_view = out_0.rearrange("(p t) j -> p t j", t=PACK)
+        out1_view = out_1[0].rearrange("p c r -> p (c r)").bitcast(I32)
+
+        def weave(src, name):
+            dst = sb.tile([P, CHUNK, PACK], BF16, name=name, align_bytes=64)
+            nc.scalar.copy(dst[:].rearrange("p (c i) t -> p c t i", i=4), src[:].rearrange("p t (c i) -> p c t i", i=4))
+            return dst
+
+        z16, acc, o, o16 = {}, {}, {}, {}
+
+        def stage_a(c):
+            curvature(PACK - 1, c)
+            z16[c] = weave(z[c], f"z16_{c}")
+
+        def stage_b(c):
+            zw = sb.tile([P, CHUNK], U32, name=f"zw{c}", align_bytes=64)
+            zs = sb.tile([P, CHUNK], U8, name=f"zs{c}", align_bytes=64)
+            nc.vector.quantize_mx(out=zw[:].bitcast(FP8X4), scales=zs[:], in_=z16[c][:].rearrange("p c t -> p (c t)"))
+            acc[c] = psum.tile([P, PACK, CHUNK], F32, name=f"acc{c}")
+            for t in range(PACK):
+                nc.tensor.matmul_mx(
+                    out=acc[c][:, t, :],
+                    lhsT=w2w[:, 2 * P * t : 2 * P * (t + 1)].bitcast(FP4X4),
+                    lhsT_scale=w2s[:, P * t : P * (t + 1)],
+                    rhs=zw[:].bitcast(FP8X4),
+                    rhs_scale=zs[:],
+                    start=True,
+                    stop=True,
+                )
+
+        def stage_c(c):
+            cols = slice(c * CHUNK, (c + 1) * CHUNK)
+            o[c] = sb.tile([P, PACK, CHUNK], F32, name=f"o{c}")
+            nc.vector.tensor_tensor(o[c][:], acc[c][:], res_sb[:, :, cols], ALU.add)
+            nc.sync.dma_start(out0_view[:, :, cols], o[c][:])
+            o16[c] = weave(o[c], f"o16_{c}")
+
+        def stage_d(c):
+            cols = slice(c * CHUNK, (c + 1) * CHUNK)
+            ow = sb.tile([P, CHUNK], U32, name=f"ow{c}", align_bytes=64)
+            nc.vector.quantize_mx(out=ow[:].bitcast(FP8X4), scales=out_scales[:, cols], in_=o16[c][:].rearrange("p c t -> p (c t)"))
+            nc.sync.dma_start(out1_view[:, cols], ow[:].bitcast(I32))
+
+        stages = (stage_a, stage_b, stage_c, stage_d)
+        for step in range(len(chunks) + len(stages) - 1):
+            for k, stage in enumerate(stages):
+                if 0 <= step - k < len(chunks):
+                    stage(step - k)
+
+        for q in range(4):
+            queue = nc.sync if q % 2 == 0 else nc.scalar
+            queue.dma_start(out_2[0, 4 * q : 4 * q + 4, :].bitcast(I32), out_scales[32 * q : 32 * q + 4, :].bitcast(I32))

@@ -37,8 +37,7 @@ def tile_picked_curvflow_none_po_kernel(tc, x_words, x_scales, w1_words, w1_scal
         xs = sb.tile([P, T], U8, name="xs", align_bytes=64)
         ww_raw = sb.tile([P, 2 * H], U8, name="ww_raw", align_bytes=64)
         ws_raw = sb.tile([P, H], U8, name="ws_raw", align_bytes=64)
-        gain = sb.tile([P, PACK], F32, name="gain")
-        warm_in = sb.tile([P, 1], F32, name="warm_in")
+        warm_in = sb.tile([P, 1], F32, name="warm_in", tag="small")
         warm_out = sb.tile([P, 1], F32, name="warm_out")
 
         def load_scales(queues, tile, src):
@@ -51,12 +50,11 @@ def tile_picked_curvflow_none_po_kernel(tc, x_words, x_scales, w1_words, w1_scal
 
         nc.sync.dma_start(offs_sb[:], offs)
         nc.sync.dma_start(rt_sb[:], rt)
-        nc.sync.dma_start(lf_sb[:], lf)
-        nc.sync.dma_start(xw[:].bitcast(I32), x_words[0].rearrange("p c r -> p (c r)").bitcast(I32))
         nc.sync.dma_start(ww_raw[:].bitcast(I32), w1_words[0].bitcast(I32))
+        nc.sync.dma_start(xw[:].bitcast(I32), x_words[0].rearrange("p c r -> p (c r)").bitcast(I32))
+        nc.sync.dma_start(lf_sb[:], lf)
         load_scales([nc.scalar] * 4, xs, x_scales)
         load_scales([nc.gpsimd, nc.gpsimd, nc.scalar, nc.scalar], ws_raw, w1_scales)
-        nc.gpsimd.dma_start(gain[:], gn.rearrange("(p t) o -> p (t o)", t=PACK))
         nc.scalar.activation(warm_out[:], warm_in[:], ACT.Abs_reciprocal_sqrt)
 
         def deal(words_raw, scales_raw, name):
@@ -66,113 +64,151 @@ def tile_picked_curvflow_none_po_kernel(tc, x_words, x_scales, w1_words, w1_scal
             nc.vector.tensor_copy(scales[:].rearrange("p (t m) -> p m t", t=PACK), scales_raw[:].rearrange("p (m t) -> p m t", t=PACK))
             return words, scales
 
-        xg = sb.tile([P, S], U32, name="xg", align_bytes=64)
+        xg = [sb.tile([P, HALF], U32, name=f"xg{h}", align_bytes=64) for h in range(2)]
         xgs = sb.tile([P, S], U8, name="xgs", align_bytes=64)
         w1w, w1s = deal(ww_raw, ws_raw, "w1")
         nc.vector.tensor_copy(xgs[:], xs[:].indirect(offs_sb[:]))
-        nc.vector.tensor_copy(xg[:], xw[:].indirect(offs_sb[:]))
+        for h in range(2):
+            nc.vector.tensor_copy(xg[h][:], xw[:].indirect(offs_sb[:, h * HALF // 16 : (h + 1) * HALF // 16]))
 
+        gain = sb.tile([P, PACK], F32, name="gain", tag="small")
+        nc.sync.dma_start(gain[:], gn.rearrange("(p t) o -> p (t o)", t=PACK))
         nc.sync.dma_start(ww_raw[:].bitcast(I32), w2_words[0].bitcast(I32))
         load_scales([nc.sync] * 4, ws_raw, w2_scales)
         res_sb = sb.tile([P, PACK, S], F32, name="res_sb", tag="big", align_bytes=64)
         nc.sync.dma_start(res_sb[:], res.rearrange("(p t) j -> p t j", t=PACK))
 
-        y_ps = [psum.tile([P, S], F32, name=f"y_ps{t}") for t in range(PACK)]
-        for t in range(PACK):
+        def product(out, words, scales, t, rhs, rhs_scale):
             nc.tensor.matmul_mx(
-                out=y_ps[t][:],
-                lhsT=w1w[:, 2 * P * t : 2 * P * (t + 1)].bitcast(FP4X4),
-                lhsT_scale=w1s[:, P * t : P * (t + 1)],
-                rhs=xg[:].bitcast(FP8X4),
-                rhs_scale=xgs[:],
+                out=out,
+                lhsT=words[:, 2 * P * t : 2 * P * (t + 1)].bitcast(FP4X4),
+                lhsT_scale=scales[:, P * t : P * (t + 1)],
+                rhs=rhs.bitcast(FP8X4),
+                rhs_scale=rhs_scale,
                 start=True,
                 stop=True,
             )
 
-        neg_gain = sb.tile([P, PACK], F32, name="neg_gain")
-        nc.vector.tensor_scalar(neg_gain[:], gain[:], -1.0, None, ALU.mult)
+        first_ps = [psum.tile([P, HALF], F32, name=f"first_ps{h}") for h in range(2)]
+        y_ps = {t: psum.tile([P, 2, HALF], F32, name=f"y_ps{t}") for t in range(1, PACK)}
+        for h in range(2):
+            for t in range(PACK):
+                product(first_ps[h][:] if t == 0 else y_ps[t][:, h, :], w1w, w1s, t, xg[h][:], xgs[:, h * HALF : (h + 1) * HALF])
 
-        y_win = [sb.tile([P, S], F32, name=f"y_win{t}") for t in range(PACK)]
-        y_own = [sb.tile([P, S], F32, name=f"y_own{t}") for t in range(PACK)]
+        y_wide = {t: sb.tile([P, 2 * S], F32, name=f"y_wide{t}") for t in (1, 2, 3)}
+        p_wide = {t: sb.tile([P, 2 * S], F32, name=f"p_wide{t}") for t in (0, 1, 2)}
+        y_first = sb.tile([P, S], F32, name="y_first")
+        p_last = sb.tile([P, S], F32, name="p_last")
+        p_tail = [sb.tile([P, S], F32, name=f"p_tail{t}") for t in (2, 3)]
+        y_win = [y_first[:]] + [y_wide[t][:, :S] for t in (1, 2, 3)]
+        y_own = [y_wide[t][:, S:] for t in (1, 2, 3)] + [p_wide[0][:, S:]]
+        p_win = [p_wide[t][:, :S] for t in (0, 1, 2)] + [p_last[:]]
+        p_own = [p_wide[t][:, S:] for t in (1, 2)] + [p_tail[0][:], p_tail[1][:]]
         d = [sb.tile([P, S], F32, name=f"d{t}") for t in range(PACK)]
         sq = [sb.tile([P, S], F32, name=f"sq{t}") for t in range(PACK)]
         r = [sb.tile([P, S], F32, name=f"r{t}") for t in range(PACK)]
-        p_win = [sb.tile([P, S], F32, name=f"p_win{t}") for t in range(PACK)]
-        p_own = [sb.tile([P, S], F32, name=f"p_own{t}") for t in range(PACK)]
-        z = [sb.tile([P, PACK, CHUNK], F32, name=f"z{c}") for c in range(S // CHUNK)]
+        z = sb.tile([P, PACK, S], F32, name="z")
 
-        def leave_psum(t):
-            nc.scalar.copy(y_win[t][:], y_ps[t][:])
-            nc.scalar.copy(y_own[t][:], y_ps[t][:])
+        def leave(dst, t):
+            nc.scalar.copy(dst[t], y_ps[t][:].rearrange("p h c -> p (h c)"))
 
         def difference(t):
+            if t > 0:
+                nc.vector.tensor_tensor(d[t][:], y_wide[t][:].indirect(rt_sb[:]), y_own[t], ALU.subtract)
+                return
             for h in range(S // HALF):
                 cols = slice(h * HALF, (h + 1) * HALF)
-                nc.vector.tensor_tensor(d[t][:, cols], y_win[t][:].indirect(rt_sb[:, h * HALF // 16 : (h + 1) * HALF // 16]), y_own[t][:, cols], ALU.subtract)
+                nc.vector.tensor_tensor(d[0][:, cols], y_first[:].indirect(rt_sb[:, h * HALF // 16 : (h + 1) * HALF // 16]), y_own[0][:, cols], ALU.subtract)
+
+        def square(t):
+            nc.scalar.activation(sq[t][:], d[t][:], ACT.Square)
 
         def root(t):
-            nc.scalar.activation(sq[t][:], d[t][:], ACT.Square)
             nc.scalar.activation(r[t][:], sq[t][:], ACT.Abs_reciprocal_sqrt, bias=1.0)
 
         def slope(t):
-            nc.vector.scalar_tensor_tensor(p_win[t][:], d[t][:], neg_gain[:, t : t + 1], r[t][:], ALU.mult, ALU.mult)
-            nc.scalar.copy(p_own[t][:], p_win[t][:])
+            nc.vector.scalar_tensor_tensor(p_win[t], d[t][:], gain[:, t : t + 1], r[t][:], ALU.mult, ALU.mult)
 
-        def curvature(t, c):
+        def second(t):
+            nc.scalar.copy(p_own[t], p_win[t])
+
+        def curvature(t):
+            nc.vector.tensor_tensor(z[:, t, :], p_wide[t][:].indirect(lf_sb[:]), p_own[t], ALU.subtract)
+
+        def last_curvature(c):
             cols = slice(c * CHUNK, (c + 1) * CHUNK)
-            nc.vector.tensor_tensor(z[c][:, t, :], p_win[t][:].indirect(lf_sb[:, c * CHUNK // 16 : (c + 1) * CHUNK // 16]), p_own[t][:, cols], ALU.subtract)
+            nc.vector.tensor_tensor(z[:, PACK - 1, cols], p_last[:].indirect(lf_sb[:, c * CHUNK // 16 : (c + 1) * CHUNK // 16]), p_own[PACK - 1][:, cols], ALU.subtract)
 
         chunks = range(S // CHUNK)
-        for step in range(PACK + 2):
-            if step < PACK:
-                leave_psum(step)
-                difference(step)
-            if 1 <= step <= PACK:
-                root(step - 1)
-                slope(step - 1)
-            if step == 2:
-                w2w, w2s = deal(ww_raw, ws_raw, "w2")
-            if 2 <= step <= PACK:
-                for c in chunks:
-                    curvature(step - 2, c)
+        for h in range(2):
+            cols = slice(h * HALF, (h + 1) * HALF)
+            nc.scalar.copy(y_win[0][:, cols], first_ps[h][:])
+            nc.scalar.copy(y_own[0][:, cols], first_ps[h][:])
+        difference(0)
+        leave(y_win, 1)
+        leave(y_own, 1)
+        difference(1)
+        leave(y_win, 2)
+        square(0)
+        leave(y_own, 2)
+        difference(2)
+        root(0)
+        slope(0)
+        leave(y_win, 3)
+        square(1)
+        leave(y_own, 3)
+        difference(3)
+        w2w, w2s = deal(ww_raw, ws_raw, "w2")
+        root(1)
+        slope(1)
+        square(2)
+        second(0)
+        root(2)
+        curvature(0)
+        slope(2)
+        square(3)
+        second(1)
+        root(3)
+        slope(3)
+        second(2)
+        second(3)
+        curvature(1)
+        curvature(2)
 
         out_scales = sb.tile([P, S], U8, name="out_scales", align_bytes=64)
         out0_view = out_0.rearrange("(p t) j -> p t j", t=PACK)
         out1_view = out_1[0].rearrange("p c r -> p (c r)").bitcast(I32)
 
-        def weave(src, name):
+        def weave(src, name, sign, on_vector=False):
             dst = sb.tile([P, CHUNK, PACK], BF16, name=name, align_bytes=64)
-            nc.scalar.copy(dst[:].rearrange("p (c i) t -> p c t i", i=4), src[:].rearrange("p t (c i) -> p c t i", i=4))
+            woven = dst[:].rearrange("p (c i) t -> p c t i", i=4)
+            rows = src.rearrange("p t (c i) -> p c t i", i=4)
+            if on_vector:
+                nc.vector.tensor_scalar(woven, rows, sign, None, ALU.mult)
+            else:
+                nc.scalar.activation(woven, rows, ACT.Copy, scale=sign)
             return dst
 
         z16, acc, o, o16 = {}, {}, {}, {}
 
         def stage_a(c):
-            curvature(PACK - 1, c)
-            z16[c] = weave(z[c], f"z16_{c}")
+            last_curvature(c)
+            z16[c] = weave(z[:, :, c * CHUNK : (c + 1) * CHUNK], f"z16_{c}", -1.0, c == len(chunks) - 1)
 
         def stage_b(c):
             zw = sb.tile([P, CHUNK], U32, name=f"zw{c}", align_bytes=64)
             zs = sb.tile([P, CHUNK], U8, name=f"zs{c}", align_bytes=64)
             nc.vector.quantize_mx(out=zw[:].bitcast(FP8X4), scales=zs[:], in_=z16[c][:].rearrange("p c t -> p (c t)"))
-            acc[c] = psum.tile([P, PACK, CHUNK], F32, name=f"acc{c}")
+            acc[c] = psum.tile([P, PACK, CHUNK], F32, name=f"acc{c}", tag="acc", bufs=3)
             for t in range(PACK):
-                nc.tensor.matmul_mx(
-                    out=acc[c][:, t, :],
-                    lhsT=w2w[:, 2 * P * t : 2 * P * (t + 1)].bitcast(FP4X4),
-                    lhsT_scale=w2s[:, P * t : P * (t + 1)],
-                    rhs=zw[:].bitcast(FP8X4),
-                    rhs_scale=zs[:],
-                    start=True,
-                    stop=True,
-                )
+                product(acc[c][:, t, :], w2w, w2s, t, zw[:], zs[:])
 
         def stage_c(c):
             cols = slice(c * CHUNK, (c + 1) * CHUNK)
             o[c] = sb.tile([P, PACK, CHUNK], F32, name=f"o{c}")
             nc.vector.tensor_tensor(o[c][:], acc[c][:], res_sb[:, :, cols], ALU.add)
             nc.sync.dma_start(out0_view[:, :, cols], o[c][:])
-            o16[c] = weave(o[c], f"o16_{c}")
+            o16[c] = weave(o[c][:], f"o16_{c}", 1.0, c == len(chunks) - 1)
 
         def stage_d(c):
             cols = slice(c * CHUNK, (c + 1) * CHUNK)
@@ -180,11 +216,19 @@ def tile_picked_curvflow_none_po_kernel(tc, x_words, x_scales, w1_words, w1_scal
             nc.vector.quantize_mx(out=ow[:].bitcast(FP8X4), scales=out_scales[:, cols], in_=o16[c][:].rearrange("p c t -> p (c t)"))
             nc.sync.dma_start(out1_view[:, cols], ow[:].bitcast(I32))
 
-        stages = (stage_a, stage_b, stage_c, stage_d)
-        for step in range(len(chunks) + len(stages) - 1):
-            for k, stage in enumerate(stages):
-                if 0 <= step - k < len(chunks):
-                    stage(step - k)
+        for c in chunks:
+            stage_a(c)
+        stage_b(0)
+        stage_b(1)
+        stage_c(0)
+        stage_b(2)
+        stage_c(1)
+        stage_b(3)
+        stage_c(2)
+        stage_d(0)
+        stage_c(3)
+        for c in chunks[1:]:
+            stage_d(c)
 
         for q in range(4):
             queue = nc.sync if q % 2 == 0 else nc.scalar

@@ -60,8 +60,8 @@ def tile_picked_curvflow_none_po_kernel(tc, x_words, x_scales, w1_words, w1_scal
         def deal(words_raw, scales_raw, name):
             words = sb.tile([P, 2 * H], U8, name=name + "w", align_bytes=64)
             scales = sb.tile([P, H], U8, name=name + "s", align_bytes=64)
-            nc.vector.tensor_copy(words[:].rearrange("p (t m b) -> p m t b", t=PACK, b=2), words_raw[:].rearrange("p (m t b) -> p m t b", t=PACK, b=2))
-            nc.vector.tensor_copy(scales[:].rearrange("p (t m) -> p m t", t=PACK), scales_raw[:].rearrange("p (m t) -> p m t", t=PACK))
+            nc.vector.tensor_copy(words[:].rearrange("p (t m b) -> p t m b", t=PACK, b=2), words_raw[:].rearrange("p (m t b) -> p t m b", t=PACK, b=2))
+            nc.vector.tensor_copy(scales[:].rearrange("p (t m) -> p t m", t=PACK), scales_raw[:].rearrange("p (m t) -> p t m", t=PACK))
             return words, scales
 
         xg = [sb.tile([P, HALF], U32, name=f"xg{h}", align_bytes=64) for h in range(2)]
@@ -193,7 +193,7 @@ def tile_picked_curvflow_none_po_kernel(tc, x_words, x_scales, w1_words, w1_scal
 
         def stage_a(c):
             last_curvature(c)
-            z16[c] = weave(z[:, :, c * CHUNK : (c + 1) * CHUNK], f"z16_{c}", -1.0, c == len(chunks) - 1)
+            z16[c] = weave(z[:, :, c * CHUNK : (c + 1) * CHUNK], f"z16_{c}", -1.0)
 
         def stage_b(c):
             zw = sb.tile([P, CHUNK], U32, name=f"zw{c}", align_bytes=64)

@@ -91,8 +91,8 @@ def tile_picked_curvflow_none_po_kernel(tc, x_words, x_scales, w1_words, w1_scal
 
         first_ps = [psum.tile([P, HALF], F32, name=f"first_ps{h}") for h in range(2)]
         y_ps = {t: psum.tile([P, 2, HALF], F32, name=f"y_ps{t}") for t in range(1, PACK)}
-        for h in range(2):
-            for t in range(PACK):
+        for t in range(PACK):
+            for h in range(2):
                 product(first_ps[h][:] if t == 0 else y_ps[t][:, h, :], w1w, w1s, t, xg[h][:], xgs[:, h * HALF : (h + 1) * HALF])
 
         y_wide = {t: sb.tile([P, 2 * S], F32, name=f"y_wide{t}") for t in (1, 2, 3)}
@@ -140,24 +140,22 @@ def tile_picked_curvflow_none_po_kernel(tc, x_words, x_scales, w1_words, w1_scal
             nc.vector.tensor_tensor(z[:, PACK - 1, cols], p_last[:].indirect(lf_sb[:, c * CHUNK // 16 : (c + 1) * CHUNK // 16]), p_own[PACK - 1][:, cols], ALU.subtract)
 
         chunks = range(S // CHUNK)
-        for h in range(2):
-            cols = slice(h * HALF, (h + 1) * HALF)
-            nc.scalar.copy(y_win[0][:, cols], first_ps[h][:])
-            nc.scalar.copy(y_own[0][:, cols], first_ps[h][:])
+        nc.scalar.copy(y_win[0][:, :HALF], first_ps[0][:])
+        nc.scalar.copy(y_own[0][:, :HALF], first_ps[0][:])
+        nc.vector.tensor_copy(y_win[0][:, HALF:], first_ps[1][:])
+        nc.vector.tensor_copy(y_own[0][:, HALF:], y_win[0][:, HALF:])
         difference(0)
-        leave(y_win, 1)
-        leave(y_own, 1)
-        difference(1)
-        leave(y_win, 2)
+        for t in (1, 2):
+            leave(y_win, t)
+            leave(y_own, t)
+            difference(t)
         square(0)
-        leave(y_own, 2)
-        difference(2)
-        root(0)
-        slope(0)
         leave(y_win, 3)
-        square(1)
+        root(0)
         leave(y_own, 3)
         difference(3)
+        slope(0)
+        square(1)
         w2w, w2s = deal(ww_raw, ws_raw, "w2")
         root(1)
         slope(1)
@@ -175,6 +173,7 @@ def tile_picked_curvflow_none_po_kernel(tc, x_words, x_scales, w1_words, w1_scal
         curvature(1)
         curvature(2)
 
+        out_words = sb.tile([P, S], U32, name="out_words", align_bytes=64)
         out_scales = sb.tile([P, S], U8, name="out_scales", align_bytes=64)
         out0_view = out_0.rearrange("(p t) j -> p t j", t=PACK)
         out1_view = out_1[0].rearrange("p c r -> p (c r)").bitcast(I32)
@@ -208,13 +207,11 @@ def tile_picked_curvflow_none_po_kernel(tc, x_words, x_scales, w1_words, w1_scal
             o[c] = sb.tile([P, PACK, CHUNK], F32, name=f"o{c}")
             nc.vector.tensor_tensor(o[c][:], acc[c][:], res_sb[:, :, cols], ALU.add)
             nc.sync.dma_start(out0_view[:, :, cols], o[c][:])
-            o16[c] = weave(o[c][:], f"o16_{c}", 1.0, c == len(chunks) - 1)
+            o16[c] = weave(o[c][:], f"o16_{c}", 1.0)
 
         def stage_d(c):
             cols = slice(c * CHUNK, (c + 1) * CHUNK)
-            ow = sb.tile([P, CHUNK], U32, name=f"ow{c}", align_bytes=64)
-            nc.vector.quantize_mx(out=ow[:].bitcast(FP8X4), scales=out_scales[:, cols], in_=o16[c][:].rearrange("p c t -> p (c t)"))
-            nc.sync.dma_start(out1_view[:, cols], ow[:].bitcast(I32))
+            nc.vector.quantize_mx(out=out_words[:, cols].bitcast(FP8X4), scales=out_scales[:, cols], in_=o16[c][:].rearrange("p c t -> p (c t)"))
 
         for c in chunks:
             stage_a(c)
@@ -230,6 +227,8 @@ def tile_picked_curvflow_none_po_kernel(tc, x_words, x_scales, w1_words, w1_scal
         for c in chunks[1:]:
             stage_d(c)
 
+        for cols in (slice(0, S - CHUNK), slice(S - CHUNK, S)):
+            nc.sync.dma_start(out1_view[:, cols], out_words[:, cols].bitcast(I32))
         for q in range(4):
             queue = nc.sync if q % 2 == 0 else nc.scalar
             queue.dma_start(out_2[0, 4 * q : 4 * q + 4, :].bitcast(I32), out_scales[32 * q : 32 * q + 4, :].bitcast(I32))

@@ -140,10 +140,10 @@ def tile_picked_curvflow_none_po_kernel(tc, x_words, x_scales, w1_words, w1_scal
             nc.vector.tensor_tensor(z[:, PACK - 1, cols], p_last[:].indirect(lf_sb[:, c * CHUNK // 16 : (c + 1) * CHUNK // 16]), p_own[PACK - 1][:, cols], ALU.subtract)
 
         chunks = range(S // CHUNK)
-        nc.scalar.copy(y_win[0][:, :HALF], first_ps[0][:])
-        nc.scalar.copy(y_own[0][:, :HALF], first_ps[0][:])
-        nc.vector.tensor_copy(y_win[0][:, HALF:], first_ps[1][:])
-        nc.vector.tensor_copy(y_own[0][:, HALF:], y_win[0][:, HALF:])
+        for h in range(2):
+            cols = slice(h * HALF, (h + 1) * HALF)
+            nc.scalar.copy(y_win[0][:, cols], first_ps[h][:])
+            nc.scalar.copy(y_own[0][:, cols], first_ps[h][:])
         difference(0)
         for t in (1, 2):
             leave(y_win, t)
@@ -207,7 +207,7 @@ def tile_picked_curvflow_none_po_kernel(tc, x_words, x_scales, w1_words, w1_scal
             o[c] = sb.tile([P, PACK, CHUNK], F32, name=f"o{c}")
             nc.vector.tensor_tensor(o[c][:], acc[c][:], res_sb[:, :, cols], ALU.add)
             nc.sync.dma_start(out0_view[:, :, cols], o[c][:])
-            o16[c] = weave(o[c][:], f"o16_{c}", 1.0)
+            o16[c] = weave(o[c][:], f"o16_{c}", 1.0, c == len(chunks) - 1)
 
         def stage_d(c):
             cols = slice(c * CHUNK, (c + 1) * CHUNK)

from contextlib import ExitStack

import concourse.mybir as mybir

K, T, S, N, H = 512, 2048, 512, 512, 512
FLOPS = 2 * K * H * S + 2 * H * N * S

F32 = mybir.dt.float32
BF16 = mybir.dt.bfloat16
I32 = mybir.dt.int32
U32 = mybir.dt.uint32
U16 = mybir.dt.uint16
U8 = mybir.dt.uint8
FP8X4 = mybir.dt.float8_e4m3fn_x4
FP4X4 = mybir.dt.float4_e2m1fn_x4
ALU = mybir.AluOpType
ACT = mybir.ActivationFunctionType

P = 128
PACK = 4
HALF = 256
CHUNK = 128


def tile_picked_curvflow_none_po_kernel(tc, x_words, x_scales, w1_words, w1_scales, gn, w2_words, w2_scales, res, offs, rt, lf, out_0, out_1, out_2):
    nc = tc.nc
    with ExitStack() as ctx:
        lists = ctx.enter_context(tc.tile_pool(name="lists", bufs=1))
        sb = ctx.enter_context(tc.tile_pool(name="sb", bufs=1))
        psum = ctx.enter_context(tc.psum_pool(name="psum", bufs=1))

        offs_sb = lists.tile([P, S // 16], U16, name="offs_sb")
        rt_sb = lists.tile([P, S // 16], U16, name="rt_sb")
        lf_sb = lists.tile([P, S // 16], U16, name="lf_sb")

        xw = sb.tile([P, T], U32, name="xw", tag="big", align_bytes=64)
        xs = sb.tile([P, T], U8, name="xs", align_bytes=64)
        ww_raw = sb.tile([P, 2 * H], U8, name="ww_raw", align_bytes=64)
        ws_raw = sb.tile([P, H], U8, name="ws_raw", align_bytes=64)
        warm_in = sb.tile([P, 1], F32, name="warm_in", tag="small")
        warm_out = sb.tile([P, 1], F32, name="warm_out")

        def load_scales(queues, tile, src):
            for q, queue in enumerate(queues):
                queue.dma_start(tile[32 * q : 32 * q + 4, :].bitcast(I32), src[0, 4 * q : 4 * q + 4, :].bitcast(I32))

        nc.vector.memset(xs[:].bitcast(I32), 0)
        nc.gpsimd.memset(ws_raw[:].bitcast(I32), 0)
        nc.vector.memset(warm_in[:], 1.0)

        nc.sync.dma_start(offs_sb[:], offs)
        nc.sync.dma_start(rt_sb[:], rt)
        nc.sync.dma_start(ww_raw[:].bitcast(I32), w1_words[0].bitcast(I32))
        nc.sync.dma_start(xw[:].bitcast(I32), x_words[0].rearrange("p c r -> p (c r)").bitcast(I32))
        nc.sync.dma_start(lf_sb[:], lf)
        load_scales([nc.scalar] * 4, xs, x_scales)
        load_scales([nc.gpsimd, nc.gpsimd, nc.scalar, nc.scalar], ws_raw, w1_scales)
        nc.scalar.activation(warm_out[:], warm_in[:], ACT.Abs_reciprocal_sqrt)

        def deal(words_raw, scales_raw, name):
            words = sb.tile([P, 2 * H], U8, name=name + "w", align_bytes=64)
            scales = sb.tile([P, H], U8, name=name + "s", align_bytes=64)
            nc.vector.tensor_copy(words[:].rearrange("p (t m b) -> p t m b", t=PACK, b=2), words_raw[:].rearrange("p (m t b) -> p t m b", t=PACK, b=2))
            nc.vector.tensor_copy(scales[:].rearrange("p (t m) -> p t m", t=PACK), scales_raw[:].rearrange("p (m t) -> p t m", t=PACK))
            return words, scales

        xg = [sb.tile([P, HALF], U32, name=f"xg{h}", align_bytes=64) for h in range(2)]
        xgs = sb.tile([P, S], U8, name="xgs", align_bytes=64)
        w1w, w1s = deal(ww_raw, ws_raw, "w1")
        nc.vector.tensor_copy(xgs[:], xs[:].indirect(offs_sb[:]))
        for h in range(2):
            nc.vector.tensor_copy(xg[h][:], xw[:].indirect(offs_sb[:, h * HALF // 16 : (h + 1) * HALF // 16]))

        gain = sb.tile([P, PACK], F32, name="gain", tag="small")
        nc.sync.dma_start(gain[:], gn.rearrange("(p t) o -> p (t o)", t=PACK))
        nc.sync.dma_start(ww_raw[:].bitcast(I32), w2_words[0].bitcast(I32))
        load_scales([nc.sync] * 4, ws_raw, w2_scales)
        res_sb = sb.tile([P, PACK, S], F32, name="res_sb", tag="big", align_bytes=64)
        nc.sync.dma_start(res_sb[:], res.rearrange("(p t) j -> p t j", t=PACK))

        def product(out, words, scales, t, rhs, rhs_scale):
            nc.tensor.matmul_mx(
                out=out,
                lhsT=words[:, 2 * P * t : 2 * P * (t + 1)].bitcast(FP4X4),
                lhsT_scale=scales[:, P * t : P * (t + 1)],
                rhs=rhs.bitcast(FP8X4),
                rhs_scale=rhs_scale,
                start=True,
                stop=True,
            )

        first_ps = [psum.tile([P, HALF], F32, name=f"first_ps{h}") for h in range(2)]
        y_ps = {t: psum.tile([P, 2, HALF], F32, name=f"y_ps{t}") for t in range(1, PACK)}
        for t in range(PACK):
            for h in range(2):
                product(first_ps[h][:] if t == 0 else y_ps[t][:, h, :], w1w, w1s, t, xg[h][:], xgs[:, h * HALF : (h + 1) * HALF])

        y_wide = {t: sb.tile([P, 2 * S], F32, name=f"y_wide{t}") for t in (1, 2, 3)}
        p_wide = {t: sb.tile([P, 2 * S], F32, name=f"p_wide{t}") for t in (0, 1, 2)}
        y_first = sb.tile([P, S], F32, name="y_first")
        p_last = sb.tile([P, S], F32, name="p_last")
        p_tail = [sb.tile([P, S], F32, name=f"p_tail{t}") for t in (2, 3)]
        y_win = [y_first[:]] + [y_wide[t][:, :S] for t in (1, 2, 3)]
        y_own = [y_wide[t][:, S:] for t in (1, 2, 3)] + [p_wide[0][:, S:]]
        p_win = [p_wide[t][:, :S] for t in (0, 1, 2)] + [p_last[:]]
        p_own = [p_wide[t][:, S:] for t in (1, 2)] + [p_tail[0][:], p_tail[1][:]]
        d = [sb.tile([P, S], F32, name=f"d{t}") for t in range(PACK)]
        sq = [sb.tile([P, S], F32, name=f"sq{t}") for t in range(PACK)]
        r = [sb.tile([P, S], F32, name=f"r{t}") for t in range(PACK)]
        z = sb.tile([P, PACK, S], F32, name="z")

        def leave(dst, t):
            nc.scalar.copy(dst[t], y_ps[t][:].rearrange("p h c -> p (h c)"))

        def difference(t):
            if t > 0:
                nc.vector.tensor_tensor(d[t][:], y_wide[t][:].indirect(rt_sb[:]), y_own[t], ALU.subtract)
                return
            for h in range(S // HALF):
                cols = slice(h * HALF, (h + 1) * HALF)
                nc.vector.tensor_tensor(d[0][:, cols], y_first[:].indirect(rt_sb[:, h * HALF // 16 : (h + 1) * HALF // 16]), y_own[0][:, cols], ALU.subtract)

        def square(t):
            nc.scalar.activation(sq[t][:], d[t][:], ACT.Square)

        def root(t):
            nc.scalar.activation(r[t][:], sq[t][:], ACT.Abs_reciprocal_sqrt, bias=1.0)

        def slope(t):
            nc.vector.scalar_tensor_tensor(p_win[t], d[t][:], gain[:, t : t + 1], r[t][:], ALU.mult, ALU.mult)

        def second(t):
            nc.scalar.copy(p_own[t], p_win[t])

        def curvature(t):
            nc.vector.tensor_tensor(z[:, t, :], p_wide[t][:].indirect(lf_sb[:]), p_own[t], ALU.subtract)

        def last_curvature(c):
            cols = slice(c * CHUNK, (c + 1) * CHUNK)
            nc.vector.tensor_tensor(z[:, PACK - 1, cols], p_last[:].indirect(lf_sb[:, c * CHUNK // 16 : (c + 1) * CHUNK // 16]), p_own[PACK - 1][:, cols], ALU.subtract)

        chunks = range(S // CHUNK)
        for h in range(2):
            cols = slice(h * HALF, (h + 1) * HALF)
            nc.scalar.copy(y_win[0][:, cols], first_ps[h][:])
            nc.scalar.copy(y_own[0][:, cols], first_ps[h][:])
        difference(0)
        for t in (1, 2):
            leave(y_win, t)
            leave(y_own, t)
            difference(t)
        square(0)
        leave(y_win, 3)
        root(0)
        leave(y_own, 3)
        difference(3)
        slope(0)
        square(1)
        w2w, w2s = deal(ww_raw, ws_raw, "w2")
        root(1)
        slope(1)
        square(2)
        second(0)
        root(2)
        curvature(0)
        slope(2)
        square(3)
        second(1)
        root(3)
        slope(3)
        second(2)
        second(3)
        curvature(1)
        curvature(2)

        out_words = sb.tile([P, S], U32, name="out_words", align_bytes=64)
        out_scales = sb.tile([P, S], U8, name="out_scales", align_bytes=64)
        out0_view = out_0.rearrange("(p t) j -> p t j", t=PACK)
        out1_view = out_1[0].rearrange("p c r -> p (c r)").bitcast(I32)

        def weave(src, name, sign, on_vector=False):
            dst = sb.tile([P, CHUNK, PACK], BF16, name=name, align_bytes=64)
            woven = dst[:].rearrange("p (c i) t -> p c t i", i=4)
            rows = src.rearrange("p t (c i) -> p c t i", i=4)
            if on_vector:
                nc.vector.tensor_scalar(woven, rows, sign, None, ALU.mult)
            else:
                nc.scalar.activation(woven, rows, ACT.Copy, scale=sign)
            return dst

        z16, acc, o, o16 = {}, {}, {}, {}

        def stage_a(c):
            last_curvature(c)
            z16[c] = weave(z[:, :, c * CHUNK : (c + 1) * CHUNK], f"z16_{c}", -1.0)

        def stage_b(c):
            zw = sb.tile([P, CHUNK], U32, name=f"zw{c}", align_bytes=64)
            zs = sb.tile([P, CHUNK], U8, name=f"zs{c}", align_bytes=64)
            nc.vector.quantize_mx(out=zw[:].bitcast(FP8X4), scales=zs[:], in_=z16[c][:].rearrange("p c t -> p (c t)"))
            acc[c] = psum.tile([P, PACK, CHUNK], F32, name=f"acc{c}", tag="acc", bufs=3)
            for t in range(PACK):
                product(acc[c][:, t, :], w2w, w2s, t, zw[:], zs[:])

        def stage_c(c):
            cols = slice(c * CHUNK, (c + 1) * CHUNK)
            o[c] = sb.tile([P, PACK, CHUNK], F32, name=f"o{c}")
            nc.vector.tensor_tensor(o[c][:], acc[c][:], res_sb[:, :, cols], ALU.add)
            nc.sync.dma_start(out0_view[:, :, cols], o[c][:])
            o16[c] = weave(o[c][:], f"o16_{c}", 1.0, c == len(chunks) - 1)

        def stage_d(c):
            cols = slice(c * CHUNK, (c + 1) * CHUNK)
            nc.vector.quantize_mx(out=out_words[:, cols].bitcast(FP8X4), scales=out_scales[:, cols], in_=o16[c][:].rearrange("p c t -> p (c t)"))

        for c in chunks:
            stage_a(c)
        stage_b(0)
        stage_b(1)
        stage_c(0)
        stage_b(2)
        stage_c(1)
        stage_b(3)
        stage_c(2)
        stage_d(0)
        stage_c(3)
        for c in chunks[1:]:
            stage_d(c)

        for cols in (slice(0, S - CHUNK), slice(S - CHUNK, S)):
            nc.sync.dma_start(out1_view[:, cols], out_words[:, cols].bitcast(I32))
        for q in range(4):
            queue = nc.sync if q % 2 == 0 else nc.scalar
            queue.dma_start(out_2[0, 4 * q : 4 * q + 4, :].bitcast(I32), out_scales[32 * q : 32 * q + 4, :].bitcast(I32))
